import numpy as np
import ml_dtypes


def mxq(x, axis, fmt="e4m3"):
    dtype, down = {"e4m3": (ml_dtypes.float8_e4m3fn, 7), "e5m2": (ml_dtypes.float8_e5m2, 14)}[fmt]
    v = np.moveaxis(np.asarray(x, np.float32).astype(ml_dtypes.bfloat16).astype(np.float64), axis, -1)
    blocks = v.reshape(v.shape[:-1] + (-1, 32))
    amax = np.abs(blocks).max(-1, keepdims=True)
    byte = np.maximum(np.where(amax > 0, np.frexp(amax)[1] - 1 + 127, 0) - down, 1)
    scale = np.exp2(byte - 127.0)
    codes = (blocks / scale).astype(np.float32).astype(dtype).astype(np.float64)
    return np.moveaxis((codes * scale).reshape(v.shape), -1, axis)


WIDE = False


def mx_kscale(k):
    if not WIDE:
        return np.ones(k)
    levels = np.array([10, -10, 5, -5, 0])
    if k % 512:
        return np.exp2(np.random.permutation(np.resize(levels, k // 32))).repeat(32)
    a = np.empty((k // 512, 16))
    for p in range(k // 512):
        a[p, :8] = np.random.permutation(np.resize(levels, 8))
        for g in range(8):
            far = levels[np.abs(levels - a[p, g]) >= 10]
            a[p, g + 8] = far[np.random.randint(len(far))]
    return np.exp2(a.ravel()).repeat(32)


def f64(x):
    return np.asarray(x).astype(np.float64)


def striped(idx):
    return np.tile(idx.reshape(-1, 16).T, (8, 1)).astype(np.uint16)


def unstriped(offs):
    return offs[:16].T.reshape(-1).astype(np.int64)


E2M1 = np.array([0.0, 0.5, 1.0, 1.5, 2.0, 3.0, 4.0, 6.0, -0.0, -0.5, -1.0, -1.5, -2.0, -3.0, -4.0, -6.0])


def pack_weight(w, fmt):
    k, n = w.shape
    w = f64(np.asarray(w, np.float32).astype(ml_dtypes.bfloat16)).reshape(k // 32, 32, n)
    amax = np.abs(w).max(1)
    if fmt == "e4m3":
        byte = np.frexp(amax)[1] - 1 + 127 - 7
    else:
        mant, ex = np.frexp(amax / 6.0)
        byte = np.where(mant > 0.5, ex, ex - 1) + 127
    byte = np.clip(np.where(amax > 0, byte, 1), 1, 254)
    scaled = (w * np.exp2(127.0 - byte)[:, None, :]).reshape(k, n).astype(np.float32)
    by_word = np.ascontiguousarray(scaled.reshape(k // 512, 128, 4, n).transpose(0, 1, 3, 2))
    if fmt == "e4m3":
        words = by_word.astype(ml_dtypes.float8_e4m3fn).view(np.uint8)
    else:
        c = by_word.astype(ml_dtypes.float4_e2m1fn).view(np.uint8) & 0xF
        words = (c[..., 0::2] | (c[..., 1::2] << 4)).reshape(k // 512, 128, 2 * n)
    return np.ascontiguousarray(words), np.ascontiguousarray(byte.astype(np.uint8).reshape(k // 512, 16, n))


def unpack_weight(words, scales, fmt):
    g, _, n = scales.shape
    words = np.ascontiguousarray(words).reshape(g, 128, n, -1)
    if fmt == "e4m3":
        vals = words.view(ml_dtypes.float8_e4m3fn).astype(np.float64)
    else:
        nib = np.empty((g, 128, n, 4), np.uint8)
        nib[..., 0::2] = words & 0xF
        nib[..., 1::2] = words >> 4
        vals = E2M1[nib]
    vals = vals * np.repeat(np.exp2(scales.astype(np.float64) - 127.0), 8, axis=1)[..., None]
    return vals.transpose(0, 1, 3, 2).reshape(g * 512, n)


def gelu(v):
    return 0.5 * v * (1.0 + np.tanh(np.sqrt(2.0 / np.pi) * (v + 0.044715 * v**3)))


def striped8(idx):
    return np.concatenate([v.reshape(-1, 16).T for v in idx]).astype(np.uint16)


def unstriped8(offs):
    return np.stack([offs[16 * g:16 * g + 16].T.reshape(-1) for g in range(8)]).astype(np.int64)


def runs(v, idx8):
    k = np.arange(v.shape[0])
    return v[k[:, None], idx8[k % 512 // 64]]


K, T, S, H, P, N, RUN, BAYS = 1536, 2048, 1024, 1024, 512, 768, 64, 8


def setup_inputs():
    n = np.random.standard_normal
    ks = mx_kscale(K)[:, None]
    u = mx_kscale(H)[:, None]
    tab_words, tab_scales = pack_weight(n((K, T)) * ks, "e4m3")
    w4_words, w4_scales = pack_weight(n((H, N)) / np.sqrt(H) / u, "e2m1")
    idx8 = np.stack([np.random.permutation(S)[:P] for _ in range(BAYS)])
    gain = np.where(n(H) < 0, -1.0, 1.0) * np.random.uniform(0.8, 2.4, H)
    return {
        "tab_words": tab_words,
        "tab_scales": tab_scales,
        "offs": striped(np.random.permutation(T)[:S]),
        "offs2": striped8(idx8),
        "w1": (0.9 * n((K, H)) / np.sqrt(K) / ks).astype(np.float32),
        "scale": np.repeat(np.random.uniform(0.6, 3.0, H // RUN), RUN).astype(np.float32),
        "thresh": np.repeat(n(H // RUN), RUN).astype(np.float32),
        "gain": (gain * u[:, 0]).astype(np.float32),
        "w2": (n((H, N)) / np.sqrt(H) / u).astype(np.float32),
        "w4_words": w4_words,
        "w4_scales": w4_scales,
    }


def reference(tab_words, tab_scales, offs, offs2, w1, scale, thresh, gain, w2, w4_words, w4_scales):
    v = unpack_weight(tab_words, tab_scales, "e4m3")[:, unstriped(offs)]
    h = mxq(f64(w1), 0, "e4m3").T @ v
    hp = runs(h, unstriped8(offs2))
    gate = 1.0 / (1.0 + np.exp(-(f64(scale)[:, None] * hp + f64(thresh)[:, None])))
    y = mxq(f64(gain)[:, None] * gate, 0, "e4m3")
    first = mxq(f64(w2), 0, "e4m3").T @ y
    second = unpack_weight(w4_words, w4_scales, "e2m1").T @ y
    return np.maximum(first, second)

@@ -1,0 +1,260 @@
+from contextlib import ExitStack
+
+import concourse.mybir as mybir
+
+K, T, S, H, M, N = 1536, 2048, 1024, 1024, 512, 768
+FLOPS = 2 * K * H * S + 2 * 2 * H * N * M
+
+F32 = mybir.dt.float32
+BF16 = mybir.dt.bfloat16
+I32 = mybir.dt.int32
+U32 = mybir.dt.uint32
+U16 = mybir.dt.uint16
+U8 = mybir.dt.uint8
+FP8X4 = mybir.dt.float8_e4m3fn_x4
+FP4X4 = mybir.dt.float4_e2m1fn_x4
+ACT = mybir.ActivationFunctionType
+ALU = mybir.AluOpType
+
+P = 128
+PACK = 4
+PASS = P * PACK
+KP = K // PASS
+HP = H // PASS
+BANK = 512
+HALF = M // 2
+NT = N // P
+
+SCALAR_SHARE = {(0, 0): 64, (1, 0): 64, (2, 0): 64}
+VECTOR_EVAC = [{(0, 1), (1, 1)}, {(0, 0)}]
+
+
+def tile_list_bay_clutter_marker_kernel(
+    tc, tab_words, tab_scales, offs, offs2, w1, scale, thresh, gain, w2, w4_words, w4_scales, out
+):
+    nc = tc.nc
+    with ExitStack() as ctx:
+        lists = ctx.enter_context(tc.tile_pool(name="lists", bufs=1))
+        keep = ctx.enter_context(tc.tile_pool(name="keep", bufs=1))
+        ring = ctx.enter_context(tc.tile_pool(name="ring", bufs=1))
+        psum = ctx.enter_context(tc.psum_pool(name="psum", bufs=1))
+
+        idx = lists.tile([P, S // 16], U16, name="idx")
+        idx2 = lists.tile([P, M // 16], U16, name="idx2")
+        nc.sync.dma_start(idx[:], offs)
+
+        tab_sc = keep.tile([P, T], U8, name="tab_sc", align_bytes=64)
+        nc.gpsimd.memset(tab_sc[:].bitcast(I32), 0)
+        for q in range(4):
+            nc.scalar.dma_start(
+                tab_sc[32 * q : 32 * q + 4 * KP, :].bitcast(I32),
+                tab_scales[:, 4 * q : 4 * q + 4, :].bitcast(I32),
+            )
+        w4_sc = keep.tile([P, HP, N], U8, name="w4_sc", align_bytes=64)
+        nc.gpsimd.memset(w4_sc[:].rearrange("p b n -> p (b n)").bitcast(I32), 0)
+
+        tab = [keep.tile([P, T], U32, name=f"tab{a}", align_bytes=64) for a in range(KP)]
+        w1_raw = {}
+
+        def load_tab(a):
+            nc.sync.dma_start(tab[a][:].bitcast(I32), tab_words[a].rearrange("p t i -> p (t i)").bitcast(I32))
+
+        def load_w1(a, b):
+            raw = ring.tile([P, PACK, PASS], F32, name="w1_raw", bufs=4)
+            rows = w1[a * PASS : (a + 1) * PASS, b * PASS : (b + 1) * PASS]
+            nc.sync.dma_start(raw[:], rows.rearrange("(p j) c -> p j c", j=PACK))
+            w1_raw[(a, b)] = raw
+
+        load_tab(0)
+        load_w1(0, 0)
+        nc.sync.dma_start(idx2[:], offs2)
+        per_row = []
+        for name, vec in (("scale_t", scale), ("thresh_t", thresh), ("gain_t", gain)):
+            t = keep.tile([P, HP, PACK], F32, name=name)
+            nc.scalar.dma_start(t[:], vec.rearrange("(b p i) -> p b i", b=HP, i=PACK))
+            per_row.append(t)
+        scale_t, thresh_t, gain_t = per_row
+        load_tab(1)
+        load_w1(1, 0)
+        load_w1(2, 0)
+        load_tab(2)
+        for a in range(KP):
+            load_w1(a, 1)
+        w2_raw = [keep.tile([P, PACK, N], F32, name=f"w2_raw{b}") for b in range(HP)]
+        w4 = keep.tile([P, HP, 2 * N], U8, name="w4", align_bytes=64)
+        nc.sync.dma_start(w2_raw[0][:], w2[0:PASS, :].rearrange("(p j) c -> p j c", j=PACK))
+        nc.sync.dma_start(w4[:].bitcast(I32), w4_words.rearrange("b p c -> p b c").bitcast(I32))
+        for q in range(4):
+            nc.sync.dma_start(
+                w4_sc[32 * q : 32 * q + 4, :, :].bitcast(I32),
+                w4_scales[:, 4 * q : 4 * q + 4, :].rearrange("b r n -> r b n").bitcast(I32),
+            )
+        nc.sync.dma_start(w2_raw[1][:], w2[PASS : 2 * PASS, :].rearrange("(p j) c -> p j c", j=PACK))
+
+        v_sc = [keep.tile([P, BANK], U8, name=f"v_sc{s}", align_bytes=64) for s in range(2)]
+        v = [[keep.tile([P, BANK], U32, name=f"v{a}_{s}", align_bytes=64) for s in range(2)] for a in range(KP)]
+        stage = [keep.tile([P, PACK * PASS], BF16, name=f"stage{a}", align_bytes=64) for a in range(KP)]
+
+        def part(s):
+            return idx[:, s * (BANK // 16) : (s + 1) * (BANK // 16)]
+
+        def gather_words(a):
+            for s in range(2):
+                nc.vector.tensor_copy(v[a][s][:], tab[a][:].indirect(part(s)))
+
+        def quantise(src, name):
+            width = src.shape[1] // PACK
+            codes = keep.tile([P, width], U32, name=f"{name}_codes", align_bytes=64)
+            scales = keep.tile([P, width], U8, name=f"{name}_scales", align_bytes=64)
+            nc.vector.quantize_mx(out=codes[:].bitcast(FP8X4), scales=scales[:], in_=src)
+            return codes, scales
+
+        def round_w1(a, b):
+            src = w1_raw[(a, b)][:].rearrange("p j (m t) -> p m j t", t=PACK)
+            dst = stage[a][:].rearrange("p (t m j) -> p m j t", t=PACK, j=PACK)
+            cut = SCALAR_SHARE.get((a, b), 0)
+            if cut > 0:
+                nc.scalar.copy(dst[:, 0:cut], src[:, 0:cut])
+            if cut < P:
+                nc.vector.tensor_copy(dst[:, cut:P], src[:, cut:P])
+
+        banks = {}
+
+        def bank_order(b):
+            if b == 0:
+                return [(i, s) for s in range(2) for i in range(PACK)]
+            return [(i, s) for i in range(PACK) for s in range(2)]
+
+        def first_stage_pass(a, b):
+            codes, scales = quantise(stage[a][:], f"w1_{a}_{b}")
+            for i, s in bank_order(b):
+                cols = slice(i * P, (i + 1) * P)
+                if a == 0:
+                    banks[(i, s)] = psum.tile([P, BANK], F32, name=f"bank{2 * i + s}")
+                nc.tensor.matmul_mx(
+                    out=banks[(i, s)][:],
+                    lhsT=codes[:, cols].bitcast(FP8X4),
+                    lhsT_scale=scales[:, cols],
+                    rhs=v[a][s][:].bitcast(FP8X4),
+                    rhs_scale=v_sc[s][4 * a : P, :],
+                    start=(a == 0),
+                    stop=(a == KP - 1),
+                )
+
+        def bring_h(b):
+            h = [keep.tile([P, S], F32, name=f"h{b}_{i}") for i in range(PACK)]
+            for i, s in bank_order(b):
+                dst = h[i][:, s * BANK : (s + 1) * BANK]
+                if (i, s) in VECTOR_EVAC[b]:
+                    nc.vector.tensor_copy(dst, banks[(i, s)][:])
+                else:
+                    nc.scalar.copy(dst, banks[(i, s)][:])
+            return h
+
+        def look(h, b, i, dst, offsets):
+            nc.scalar.activation(
+                out=dst,
+                in_=h[:].indirect(offsets),
+                func=ACT.Sigmoid,
+                bias=thresh_t[:, b, i : i + 1],
+                scale=scale_t[:, b, i : i + 1],
+            )
+
+        def round_y(b, gate, y):
+            nc.vector.tensor_tensor(
+                y.rearrange("p (c e i) -> p c i e", e=4, i=PACK),
+                gate.rearrange("p i (c e) -> p c i e", e=4),
+                gain_t[:, b, :].unsqueeze(1).unsqueeze(3).to_broadcast([P, HALF // 4, PACK, 4]),
+                ALU.mult,
+            )
+
+        w2_stage = [stage[g][:, 0 : N // 2 * PACK] for g in range(2)]
+        y_stage = [stage[2][:, u * HALF * PACK : (u + 1) * HALF * PACK] for u in range(2)]
+        y_last = stage[0][:, 0 : HALF * PACK]
+
+        def round_w2(b, g):
+            nc.vector.tensor_copy(
+                w2_stage[g].rearrange("p (c e j) -> p c j e", e=4, j=PACK),
+                w2_raw[b][:, :, g * (N // 2) : (g + 1) * (N // 2)].rearrange("p j (c e) -> p c j e", e=4),
+            )
+
+        for s in range(2):
+            nc.vector.tensor_copy(v_sc[s][:], tab_sc[:].indirect(part(s)))
+        gather_words(0)
+        round_w1(0, 0)
+        first_stage_pass(0, 0)
+        gather_words(1)
+        round_w1(1, 0)
+        first_stage_pass(1, 0)
+        round_w1(2, 0)
+        gather_words(2)
+        first_stage_pass(2, 0)
+
+        round_w1(0, 1)
+        h = bring_h(0)
+        gate0 = keep.tile([P, PACK, M], F32, name="gate0")
+        for i in range(PACK):
+            look(h[i], 0, i, gate0[:, i, :], idx2[:])
+        first_stage_pass(0, 1)
+        for a in range(1, KP):
+            round_w1(a, 1)
+            first_stage_pass(a, 1)
+        h = bring_h(1)
+        gate1 = [keep.tile([P, PACK, HALF], F32, name=f"gate1_{u}") for u in range(2)]
+        for u in range(2):
+            for i in range(PACK):
+                look(h[i], 1, i, gate1[u][:, i, :], idx2[:, u * (HALF // 16) : (u + 1) * (HALF // 16)])
+
+        w2_q, y_q = {}, {}
+        for g in range(2):
+            round_w2(0, g)
+        for g in range(2):
+            w2_q[(0, g)] = quantise(w2_stage[g], f"w2_0_{g}")
+        round_y(0, gate0[:, :, 0:HALF], y_stage[0])
+        round_w2(1, 0)
+        y_q[(0, 0)] = quantise(y_stage[0], "y_0_0")
+        round_w2(1, 1)
+        w2_q[(1, 0)] = quantise(w2_stage[0], "w2_1_0")
+        round_y(0, gate0[:, :, HALF:M], y_stage[1])
+        w2_q[(1, 1)] = quantise(w2_stage[1], "w2_1_1")
+        y_q[(0, 1)] = quantise(y_stage[1], "y_0_1")
+
+        def second_stage_pass(acc, b, u, n):
+            y_codes, y_scales = y_q[(b, u)]
+            codes, scales = w2_q[(b, n // 3)]
+            cols = slice((n % 3) * P, (n % 3 + 1) * P)
+            nc.tensor.matmul_mx(
+                out=acc[:, 0, :],
+                lhsT=w4[:, b, 2 * n * P : 2 * (n + 1) * P].bitcast(FP4X4),
+                lhsT_scale=w4_sc[:, b, n * P : (n + 1) * P],
+                rhs=y_codes[:].bitcast(FP8X4),
+                rhs_scale=y_scales[:],
+                start=(b == 0),
+                stop=False,
+            )
+            nc.tensor.matmul_mx(
+                out=acc[:, 1, :],
+                lhsT=codes[:, cols].bitcast(FP8X4),
+                lhsT_scale=scales[:, cols],
+                rhs=y_codes[:].bitcast(FP8X4),
+                rhs_scale=y_scales[:],
+                start=False,
+                stop=(b == HP - 1),
+            )
+
+        for u in range(2):
+            round_y(1, gate1[u][:], y_last)
+            y_q[(1, u)] = quantise(y_last, f"y_1_{u}")
+            accs = [psum.tile([P, 2, HALF], F32, name=f"bank{(u * NT + n) % 8}") for n in range(NT)]
+            for b in range(HP):
+                for n in range(NT):
+                    second_stage_pass(accs[n], b, u, n)
+            for n2 in range(NT // 2):
+                res = ring.tile([P, 2, HALF], F32, name="res", bufs=6)
+                for d in range(2):
+                    acc = accs[2 * n2 + d]
+                    side = ring.tile([P, HALF], F32, name="side", bufs=3)
+                    nc.scalar.copy(side[:], acc[:, 0, :])
+                    nc.vector.tensor_tensor(res[:, d, :], acc[:, 1, :], side[:], ALU.max)
+                rows = out[2 * n2 * P : 2 * (n2 + 1) * P, u * HALF : (u + 1) * HALF]
+                nc.sync.dma_start(rows.rearrange("(d p) m -> p d m", p=P), res[:])

@@ -50,6 +50,9 @@ def tile_list_bay_clutter_marker_kernel(
                 tab_sc[32 * q : 32 * q + 4 * KP, :].bitcast(I32),
                 tab_scales[:, 4 * q : 4 * q + 4, :].bitcast(I32),
             )
+        warm = keep.tile([P, 2], F32, name="warm")
+        nc.gpsimd.memset(warm[:], 0.0)
+        nc.scalar.activation(out=warm[:, 1:2], in_=warm[:, 0:1], func=ACT.Sigmoid)
         w4_sc = keep.tile([P, HP, N], U8, name="w4_sc", align_bytes=64)
         nc.gpsimd.memset(w4_sc[:].rearrange("p b n -> p (b n)").bitcast(I32), 0)
 

@@ -25,8 +25,8 @@ BANK = 512
 HALF = M // 2
 NT = N // P
 
-SCALAR_SHARE = {(0, 0): 64, (1, 0): 64, (2, 0): 64}
-VECTOR_EVAC = [{(0, 1), (1, 1)}, {(0, 0)}]
+SCALAR_SHARE = {(0, 0): 2, (1, 0): 1, (2, 0): 1}
+VECTOR_EVAC = [{(0, 1), (1, 1)}, set()]
 
 
 def tile_list_bay_clutter_marker_kernel(
@@ -46,7 +46,7 @@ def tile_list_bay_clutter_marker_kernel(
         tab_sc = keep.tile([P, T], U8, name="tab_sc", align_bytes=64)
         nc.gpsimd.memset(tab_sc[:].bitcast(I32), 0)
         for q in range(4):
-            nc.scalar.dma_start(
+            nc.gpsimd.dma_start(
                 tab_sc[32 * q : 32 * q + 4 * KP, :].bitcast(I32),
                 tab_scales[:, 4 * q : 4 * q + 4, :].bitcast(I32),
             )
@@ -86,13 +86,13 @@ def tile_list_bay_clutter_marker_kernel(
         w2_raw = [keep.tile([P, PACK, N], F32, name=f"w2_raw{b}") for b in range(HP)]
         w4 = keep.tile([P, HP, 2 * N], U8, name="w4", align_bytes=64)
         nc.sync.dma_start(w2_raw[0][:], w2[0:PASS, :].rearrange("(p j) c -> p j c", j=PACK))
+        nc.sync.dma_start(w2_raw[1][:], w2[PASS : 2 * PASS, :].rearrange("(p j) c -> p j c", j=PACK))
         nc.sync.dma_start(w4[:].bitcast(I32), w4_words.rearrange("b p c -> p b c").bitcast(I32))
         for q in range(4):
             nc.sync.dma_start(
                 w4_sc[32 * q : 32 * q + 4, :, :].bitcast(I32),
                 w4_scales[:, 4 * q : 4 * q + 4, :].rearrange("b r n -> r b n").bitcast(I32),
             )
-        nc.sync.dma_start(w2_raw[1][:], w2[PASS : 2 * PASS, :].rearrange("(p j) c -> p j c", j=PACK))
 
         v_sc = [keep.tile([P, BANK], U8, name=f"v_sc{s}", align_bytes=64) for s in range(2)]
         v = [[keep.tile([P, BANK], U32, name=f"v{a}_{s}", align_bytes=64) for s in range(2)] for a in range(KP)]
@@ -115,11 +115,12 @@ def tile_list_bay_clutter_marker_kernel(
         def round_w1(a, b):
             src = w1_raw[(a, b)][:].rearrange("p j (m t) -> p m j t", t=PACK)
             dst = stage[a][:].rearrange("p (t m j) -> p m j t", t=PACK, j=PACK)
-            cut = SCALAR_SHARE.get((a, b), 0)
-            if cut > 0:
-                nc.scalar.copy(dst[:, 0:cut], src[:, 0:cut])
-            if cut < P:
-                nc.vector.tensor_copy(dst[:, cut:P], src[:, cut:P])
+            for pair in range(2):
+                t2 = slice(2 * pair, 2 * pair + 2)
+                if pair >= 2 - SCALAR_SHARE.get((a, b), 0):
+                    nc.scalar.copy(dst[:, :, :, t2], src[:, :, :, t2])
+                else:
+                    nc.vector.tensor_copy(dst[:, :, :, t2], src[:, :, :, t2])
 
         banks = {}
 
@@ -129,9 +130,10 @@ def tile_list_bay_clutter_marker_kernel(
             return [(i, s) for i in range(PACK) for s in range(2)]
 
         def first_stage_pass(a, b):
-            codes, scales = quantise(stage[a][:], f"w1_{a}_{b}")
+            pairs = [quantise(stage[a][:, d * 2 * PASS : (d + 1) * 2 * PASS], f"w1_{a}_{b}_{d}") for d in range(2)]
             for i, s in bank_order(b):
-                cols = slice(i * P, (i + 1) * P)
+                codes, scales = pairs[i // 2]
+                cols = slice((i % 2) * P, (i % 2 + 1) * P)
                 if a == 0:
                     banks[(i, s)] = psum.tile([P, BANK], F32, name=f"bank{2 * i + s}")
                 nc.tensor.matmul_mx(
@@ -165,9 +167,9 @@ def tile_list_bay_clutter_marker_kernel(
 
         def round_y(b, gate, y):
             nc.vector.tensor_tensor(
-                y.rearrange("p (c e i) -> p c i e", e=4, i=PACK),
-                gate.rearrange("p i (c e) -> p c i e", e=4),
-                gain_t[:, b, :].unsqueeze(1).unsqueeze(3).to_broadcast([P, HALF // 4, PACK, 4]),
+                y.rearrange("p (c e i) -> p c i e", e=2, i=PACK),
+                gate.rearrange("p i (c e) -> p c i e", e=2),
+                gain_t[:, b, :].unsqueeze(1).unsqueeze(3).to_broadcast([P, HALF // 2, PACK, 2]),
                 ALU.mult,
             )
 
@@ -181,9 +183,9 @@ def tile_list_bay_clutter_marker_kernel(
                 w2_raw[b][:, :, g * (N // 2) : (g + 1) * (N // 2)].rearrange("p j (c e) -> p c j e", e=4),
             )
 
+        gather_words(0)
         for s in range(2):
             nc.vector.tensor_copy(v_sc[s][:], tab_sc[:].indirect(part(s)))
-        gather_words(0)
         round_w1(0, 0)
         first_stage_pass(0, 0)
         gather_words(1)

@@ -26,6 +26,7 @@ HALF = M // 2
 NT = N // P
 
 SCALAR_SHARE = {(0, 0): 2, (1, 0): 1, (2, 0): 1}
+STORES = [[(0, 2), (2, 2), (4, 2)], [(0, 2), (2, 2), (4, 1), (5, 1)]]
 VECTOR_EVAC = [{(0, 1), (1, 1)}, set()]
 
 
@@ -51,10 +52,10 @@ def tile_list_bay_clutter_marker_kernel(
                 tab_scales[:, 4 * q : 4 * q + 4, :].bitcast(I32),
             )
         warm = keep.tile([P, 2], F32, name="warm")
-        nc.gpsimd.memset(warm[:], 0.0)
+        nc.vector.memset(warm[:], 0.0)
         nc.scalar.activation(out=warm[:, 1:2], in_=warm[:, 0:1], func=ACT.Sigmoid)
         w4_sc = keep.tile([P, HP, N], U8, name="w4_sc", align_bytes=64)
-        nc.gpsimd.memset(w4_sc[:].rearrange("p b n -> p (b n)").bitcast(I32), 0)
+        nc.vector.memset(w4_sc[:].rearrange("p b n -> p (b n)").bitcast(I32), 0)
 
         tab = [keep.tile([P, T], U32, name=f"tab{a}", align_bytes=64) for a in range(KP)]
         w1_raw = {}
@@ -70,19 +71,26 @@ def tile_list_bay_clutter_marker_kernel(
 
         load_tab(0)
         load_w1(0, 0)
-        nc.sync.dma_start(idx2[:], offs2)
-        per_row = []
-        for name, vec in (("scale_t", scale), ("thresh_t", thresh), ("gain_t", gain)):
-            t = keep.tile([P, HP, PACK], F32, name=name)
-            nc.scalar.dma_start(t[:], vec.rearrange("(b p i) -> p b i", b=HP, i=PACK))
-            per_row.append(t)
-        scale_t, thresh_t, gain_t = per_row
         load_tab(1)
         load_w1(1, 0)
         load_w1(2, 0)
         load_tab(2)
-        for a in range(KP):
-            load_w1(a, 1)
+
+        def load_rows(vec, b, name):
+            t = keep.tile([P, PACK], F32, name=f"{name}{b}")
+            nc.sync.dma_start(t[:], vec[b * PASS : (b + 1) * PASS].rearrange("(p i) -> p i", i=PACK))
+            return t
+
+        load_w1(0, 1)
+        nc.sync.dma_start(idx2[:], offs2)
+        scale_t = [load_rows(scale, 0, "scale")]
+        thresh_t = [load_rows(thresh, 0, "thresh")]
+        load_w1(1, 1)
+        load_w1(2, 1)
+        gain_t = keep.tile([P, HP, PACK], F32, name="gain_t")
+        nc.sync.dma_start(gain_t[:], gain.rearrange("(b p i) -> p b i", b=HP, i=PACK))
+        scale_t.append(load_rows(scale, 1, "scale"))
+        thresh_t.append(load_rows(thresh, 1, "thresh"))
         w2_raw = [keep.tile([P, PACK, N], F32, name=f"w2_raw{b}") for b in range(HP)]
         w4 = keep.tile([P, HP, 2 * N], U8, name="w4", align_bytes=64)
         nc.sync.dma_start(w2_raw[0][:], w2[0:PASS, :].rearrange("(p j) c -> p j c", j=PACK))
@@ -161,8 +169,8 @@ def tile_list_bay_clutter_marker_kernel(
                 out=dst,
                 in_=h[:].indirect(offsets),
                 func=ACT.Sigmoid,
-                bias=thresh_t[:, b, i : i + 1],
-                scale=scale_t[:, b, i : i + 1],
+                bias=thresh_t[b][:, i : i + 1],
+                scale=scale_t[b][:, i : i + 1],
             )
 
         def round_y(b, gate, y):
@@ -211,18 +219,20 @@ def tile_list_bay_clutter_marker_kernel(
                 look(h[i], 1, i, gate1[u][:, i, :], idx2[:, u * (HALF // 16) : (u + 1) * (HALF // 16)])
 
         w2_q, y_q = {}, {}
+        for u in range(2):
+            round_y(0, gate0[:, :, u * HALF : (u + 1) * HALF], y_stage[u])
+            if u == 1:
+                w2_q[(0, 1)] = quantise(w2_stage[1], "w2_0_1")
+                y_q[(0, 1)] = quantise(y_stage[1], "y_0_1")
+            else:
+                round_w2(0, 0)
+                y_q[(0, 0)] = quantise(y_stage[0], "y_0_0")
+                round_w2(0, 1)
+                w2_q[(0, 0)] = quantise(w2_stage[0], "w2_0_0")
         for g in range(2):
-            round_w2(0, g)
+            round_w2(1, g)
         for g in range(2):
-            w2_q[(0, g)] = quantise(w2_stage[g], f"w2_0_{g}")
-        round_y(0, gate0[:, :, 0:HALF], y_stage[0])
-        round_w2(1, 0)
-        y_q[(0, 0)] = quantise(y_stage[0], "y_0_0")
-        round_w2(1, 1)
-        w2_q[(1, 0)] = quantise(w2_stage[0], "w2_1_0")
-        round_y(0, gate0[:, :, HALF:M], y_stage[1])
-        w2_q[(1, 1)] = quantise(w2_stage[1], "w2_1_1")
-        y_q[(0, 1)] = quantise(y_stage[1], "y_0_1")
+            w2_q[(1, g)] = quantise(w2_stage[g], f"w2_1_{g}")
 
         def second_stage_pass(acc, b, u, n):
             y_codes, y_scales = y_q[(b, u)]
@@ -254,12 +264,12 @@ def tile_list_bay_clutter_marker_kernel(
             for b in range(HP):
                 for n in range(NT):
                     second_stage_pass(accs[n], b, u, n)
-            for n2 in range(NT // 2):
-                res = ring.tile([P, 2, HALF], F32, name="res", bufs=6)
-                for d in range(2):
-                    acc = accs[2 * n2 + d]
+            for first, count in STORES[u]:
+                res = ring.tile([P, count, HALF], F32, name="res", bufs=7)
+                for d in range(count):
+                    acc = accs[first + d]
                     side = ring.tile([P, HALF], F32, name="side", bufs=3)
                     nc.scalar.copy(side[:], acc[:, 0, :])
                     nc.vector.tensor_tensor(res[:, d, :], acc[:, 1, :], side[:], ALU.max)
-                rows = out[2 * n2 * P : 2 * (n2 + 1) * P, u * HALF : (u + 1) * HALF]
+                rows = out[first * P : (first + count) * P, u * HALF : (u + 1) * HALF]
                 nc.sync.dma_start(rows.rearrange("(d p) m -> p d m", p=P), res[:])

@@ -47,15 +47,15 @@ def tile_list_bay_clutter_marker_kernel(
         tab_sc = keep.tile([P, T], U8, name="tab_sc", align_bytes=64)
         nc.gpsimd.memset(tab_sc[:].bitcast(I32), 0)
         for q in range(4):
-            nc.gpsimd.dma_start(
+            nc.scalar.dma_start(
                 tab_sc[32 * q : 32 * q + 4 * KP, :].bitcast(I32),
                 tab_scales[:, 4 * q : 4 * q + 4, :].bitcast(I32),
             )
         warm = keep.tile([P, 2], F32, name="warm")
-        nc.vector.memset(warm[:], 0.0)
+        nc.gpsimd.memset(warm[:], 0.0)
         nc.scalar.activation(out=warm[:, 1:2], in_=warm[:, 0:1], func=ACT.Sigmoid)
         w4_sc = keep.tile([P, HP, N], U8, name="w4_sc", align_bytes=64)
-        nc.vector.memset(w4_sc[:].rearrange("p b n -> p (b n)").bitcast(I32), 0)
+        nc.gpsimd.memset(w4_sc[:].rearrange("p b n -> p (b n)").bitcast(I32), 0)
 
         tab = [keep.tile([P, T], U32, name=f"tab{a}", align_bytes=64) for a in range(KP)]
         w1_raw = {}
@@ -69,28 +69,27 @@ def tile_list_bay_clutter_marker_kernel(
             nc.sync.dma_start(raw[:], rows.rearrange("(p j) c -> p j c", j=PACK))
             w1_raw[(a, b)] = raw
 
+        def load_rows(vec, b, name, queue):
+            t = keep.tile([P, PACK], F32, name=f"{name}{b}")
+            queue.dma_start(t[:], vec[b * PASS : (b + 1) * PASS].rearrange("(p i) -> p i", i=PACK))
+            return t
+
         load_tab(0)
         load_w1(0, 0)
+        nc.sync.dma_start(idx2[:], offs2)
+        scale_t = [load_rows(scale, 0, "scale", nc.scalar)]
+        thresh_t = [load_rows(thresh, 0, "thresh", nc.scalar)]
         load_tab(1)
         load_w1(1, 0)
         load_w1(2, 0)
         load_tab(2)
-
-        def load_rows(vec, b, name):
-            t = keep.tile([P, PACK], F32, name=f"{name}{b}")
-            nc.sync.dma_start(t[:], vec[b * PASS : (b + 1) * PASS].rearrange("(p i) -> p i", i=PACK))
-            return t
-
         load_w1(0, 1)
-        nc.sync.dma_start(idx2[:], offs2)
-        scale_t = [load_rows(scale, 0, "scale")]
-        thresh_t = [load_rows(thresh, 0, "thresh")]
         load_w1(1, 1)
         load_w1(2, 1)
         gain_t = keep.tile([P, HP, PACK], F32, name="gain_t")
         nc.sync.dma_start(gain_t[:], gain.rearrange("(b p i) -> p b i", b=HP, i=PACK))
-        scale_t.append(load_rows(scale, 1, "scale"))
-        thresh_t.append(load_rows(thresh, 1, "thresh"))
+        scale_t.append(load_rows(scale, 1, "scale", nc.sync))
+        thresh_t.append(load_rows(thresh, 1, "thresh", nc.sync))
         w2_raw = [keep.tile([P, PACK, N], F32, name=f"w2_raw{b}") for b in range(HP)]
         w4 = keep.tile([P, HP, 2 * N], U8, name="w4", align_bytes=64)
         nc.sync.dma_start(w2_raw[0][:], w2[0:PASS, :].rearrange("(p j) c -> p j c", j=PACK))
@@ -191,9 +190,9 @@ def tile_list_bay_clutter_marker_kernel(
                 w2_raw[b][:, :, g * (N // 2) : (g + 1) * (N // 2)].rearrange("p j (c e) -> p c j e", e=4),
             )
 
-        gather_words(0)
         for s in range(2):
             nc.vector.tensor_copy(v_sc[s][:], tab_sc[:].indirect(part(s)))
+        gather_words(0)
         round_w1(0, 0)
         first_stage_pass(0, 0)
         gather_words(1)

from contextlib import ExitStack

import concourse.mybir as mybir

K, T, S, H, M, N = 1536, 2048, 1024, 1024, 512, 768
FLOPS = 2 * K * H * S + 2 * 2 * H * N * M

F32 = mybir.dt.float32
BF16 = mybir.dt.bfloat16
I32 = mybir.dt.int32
U32 = mybir.dt.uint32
U16 = mybir.dt.uint16
U8 = mybir.dt.uint8
FP8X4 = mybir.dt.float8_e4m3fn_x4
FP4X4 = mybir.dt.float4_e2m1fn_x4
ACT = mybir.ActivationFunctionType
ALU = mybir.AluOpType

P = 128
PACK = 4
PASS = P * PACK
KP = K // PASS
HP = H // PASS
BANK = 512
HALF = M // 2
NT = N // P

SCALAR_SHARE = {(0, 0): 2, (1, 0): 1, (2, 0): 1}
STORES = [[(0, 2), (2, 2), (4, 2)], [(0, 2), (2, 2), (4, 1), (5, 1)]]
VECTOR_EVAC = [{(0, 1), (1, 1)}, set()]


def tile_list_bay_clutter_marker_kernel(
    tc, tab_words, tab_scales, offs, offs2, w1, scale, thresh, gain, w2, w4_words, w4_scales, out
):
    nc = tc.nc
    with ExitStack() as ctx:
        lists = ctx.enter_context(tc.tile_pool(name="lists", bufs=1))
        keep = ctx.enter_context(tc.tile_pool(name="keep", bufs=1))
        ring = ctx.enter_context(tc.tile_pool(name="ring", bufs=1))
        psum = ctx.enter_context(tc.psum_pool(name="psum", bufs=1))

        idx = lists.tile([P, S // 16], U16, name="idx")
        idx2 = lists.tile([P, M // 16], U16, name="idx2")
        nc.sync.dma_start(idx[:], offs)

        tab_sc = keep.tile([P, T], U8, name="tab_sc", align_bytes=64)
        nc.gpsimd.memset(tab_sc[:].bitcast(I32), 0)
        for q in range(4):
            nc.scalar.dma_start(
                tab_sc[32 * q : 32 * q + 4 * KP, :].bitcast(I32),
                tab_scales[:, 4 * q : 4 * q + 4, :].bitcast(I32),
            )
        warm = keep.tile([P, 2], F32, name="warm")
        nc.gpsimd.memset(warm[:], 0.0)
        nc.scalar.activation(out=warm[:, 1:2], in_=warm[:, 0:1], func=ACT.Sigmoid)
        w4_sc = keep.tile([P, HP, N], U8, name="w4_sc", align_bytes=64)
        nc.gpsimd.memset(w4_sc[:].rearrange("p b n -> p (b n)").bitcast(I32), 0)

        tab = [keep.tile([P, T], U32, name=f"tab{a}", align_bytes=64) for a in range(KP)]
        w1_raw = {}

        def load_tab(a):
            nc.sync.dma_start(tab[a][:].bitcast(I32), tab_words[a].rearrange("p t i -> p (t i)").bitcast(I32))

        def load_w1(a, b):
            raw = ring.tile([P, PACK, PASS], F32, name="w1_raw", bufs=4)
            rows = w1[a * PASS : (a + 1) * PASS, b * PASS : (b + 1) * PASS]
            nc.sync.dma_start(raw[:], rows.rearrange("(p j) c -> p j c", j=PACK))
            w1_raw[(a, b)] = raw

        def load_rows(vec, b, name, queue):
            t = keep.tile([P, PACK], F32, name=f"{name}{b}")
            queue.dma_start(t[:], vec[b * PASS : (b + 1) * PASS].rearrange("(p i) -> p i", i=PACK))
            return t

        load_tab(0)
        load_w1(0, 0)
        nc.sync.dma_start(idx2[:], offs2)
        scale_t = [load_rows(scale, 0, "scale", nc.scalar)]
        thresh_t = [load_rows(thresh, 0, "thresh", nc.scalar)]
        load_tab(1)
        load_w1(1, 0)
        load_w1(2, 0)
        load_tab(2)
        load_w1(0, 1)
        load_w1(1, 1)
        load_w1(2, 1)
        gain_t = keep.tile([P, HP, PACK], F32, name="gain_t")
        nc.sync.dma_start(gain_t[:], gain.rearrange("(b p i) -> p b i", b=HP, i=PACK))
        scale_t.append(load_rows(scale, 1, "scale", nc.sync))
        thresh_t.append(load_rows(thresh, 1, "thresh", nc.sync))
        w2_raw = [keep.tile([P, PACK, N], F32, name=f"w2_raw{b}") for b in range(HP)]
        w4 = keep.tile([P, HP, 2 * N], U8, name="w4", align_bytes=64)
        nc.sync.dma_start(w2_raw[0][:], w2[0:PASS, :].rearrange("(p j) c -> p j c", j=PACK))
        nc.sync.dma_start(w2_raw[1][:], w2[PASS : 2 * PASS, :].rearrange("(p j) c -> p j c", j=PACK))
        nc.sync.dma_start(w4[:].bitcast(I32), w4_words.rearrange("b p c -> p b c").bitcast(I32))
        for q in range(4):
            nc.sync.dma_start(
                w4_sc[32 * q : 32 * q + 4, :, :].bitcast(I32),
                w4_scales[:, 4 * q : 4 * q + 4, :].rearrange("b r n -> r b n").bitcast(I32),
            )

        v_sc = [keep.tile([P, BANK], U8, name=f"v_sc{s}", align_bytes=64) for s in range(2)]
        v = [[keep.tile([P, BANK], U32, name=f"v{a}_{s}", align_bytes=64) for s in range(2)] for a in range(KP)]
        stage = [keep.tile([P, PACK * PASS], BF16, name=f"stage{a}", align_bytes=64) for a in range(KP)]

        def part(s):
            return idx[:, s * (BANK // 16) : (s + 1) * (BANK // 16)]

        def gather_words(a):
            for s in range(2):
                nc.vector.tensor_copy(v[a][s][:], tab[a][:].indirect(part(s)))

        def quantise(src, name):
            width = src.shape[1] // PACK
            codes = keep.tile([P, width], U32, name=f"{name}_codes", align_bytes=64)
            scales = keep.tile([P, width], U8, name=f"{name}_scales", align_bytes=64)
            nc.vector.quantize_mx(out=codes[:].bitcast(FP8X4), scales=scales[:], in_=src)
            return codes, scales

        def round_w1(a, b):
            src = w1_raw[(a, b)][:].rearrange("p j (m t) -> p m j t", t=PACK)
            dst = stage[a][:].rearrange("p (t m j) -> p m j t", t=PACK, j=PACK)
            for pair in range(2):
                t2 = slice(2 * pair, 2 * pair + 2)
                if pair >= 2 - SCALAR_SHARE.get((a, b), 0):
                    nc.scalar.copy(dst[:, :, :, t2], src[:, :, :, t2])
                else:
                    nc.vector.tensor_copy(dst[:, :, :, t2], src[:, :, :, t2])

        banks = {}

        def bank_order(b):
            if b == 0:
                return [(i, s) for s in range(2) for i in range(PACK)]
            return [(i, s) for i in range(PACK) for s in range(2)]

        def first_stage_pass(a, b):
            pairs = [quantise(stage[a][:, d * 2 * PASS : (d + 1) * 2 * PASS], f"w1_{a}_{b}_{d}") for d in range(2)]
            for i, s in bank_order(b):
                codes, scales = pairs[i // 2]
                cols = slice((i % 2) * P, (i % 2 + 1) * P)
                if a == 0:
                    banks[(i, s)] = psum.tile([P, BANK], F32, name=f"bank{2 * i + s}")
                nc.tensor.matmul_mx(
                    out=banks[(i, s)][:],
                    lhsT=codes[:, cols].bitcast(FP8X4),
                    lhsT_scale=scales[:, cols],
                    rhs=v[a][s][:].bitcast(FP8X4),
                    rhs_scale=v_sc[s][4 * a : P, :],
                    start=(a == 0),
                    stop=(a == KP - 1),
                )

        def bring_h(b):
            h = [keep.tile([P, S], F32, name=f"h{b}_{i}") for i in range(PACK)]
            for i, s in bank_order(b):
                dst = h[i][:, s * BANK : (s + 1) * BANK]
                if (i, s) in VECTOR_EVAC[b]:
                    nc.vector.tensor_copy(dst, banks[(i, s)][:])
                else:
                    nc.scalar.copy(dst, banks[(i, s)][:])
            return h

        def look(h, b, i, dst, offsets):
            nc.scalar.activation(
                out=dst,
                in_=h[:].indirect(offsets),
                func=ACT.Sigmoid,
                bias=thresh_t[b][:, i : i + 1],
                scale=scale_t[b][:, i : i + 1],
            )

        def round_y(b, gate, y):
            nc.vector.tensor_tensor(
                y.rearrange("p (c e i) -> p c i e", e=2, i=PACK),
                gate.rearrange("p i (c e) -> p c i e", e=2),
                gain_t[:, b, :].unsqueeze(1).unsqueeze(3).to_broadcast([P, HALF // 2, PACK, 2]),
                ALU.mult,
            )

        w2_stage = [stage[g][:, 0 : N // 2 * PACK] for g in range(2)]
        y_stage = [stage[2][:, u * HALF * PACK : (u + 1) * HALF * PACK] for u in range(2)]
        y_last = stage[0][:, 0 : HALF * PACK]

        def round_w2(b, g):
            nc.vector.tensor_copy(
                w2_stage[g].rearrange("p (c e j) -> p c j e", e=4, j=PACK),
                w2_raw[b][:, :, g * (N // 2) : (g + 1) * (N // 2)].rearrange("p j (c e) -> p c j e", e=4),
            )

        for s in range(2):
            nc.vector.tensor_copy(v_sc[s][:], tab_sc[:].indirect(part(s)))
        gather_words(0)
        round_w1(0, 0)
        first_stage_pass(0, 0)
        gather_words(1)
        round_w1(1, 0)
        first_stage_pass(1, 0)
        round_w1(2, 0)
        gather_words(2)
        first_stage_pass(2, 0)

        round_w1(0, 1)
        h = bring_h(0)
        gate0 = keep.tile([P, PACK, M], F32, name="gate0")
        for i in range(PACK):
            look(h[i], 0, i, gate0[:, i, :], idx2[:])
        first_stage_pass(0, 1)
        for a in range(1, KP):
            round_w1(a, 1)
            first_stage_pass(a, 1)
        h = bring_h(1)
        gate1 = [keep.tile([P, PACK, HALF], F32, name=f"gate1_{u}") for u in range(2)]
        for u in range(2):
            for i in range(PACK):
                look(h[i], 1, i, gate1[u][:, i, :], idx2[:, u * (HALF // 16) : (u + 1) * (HALF // 16)])

        w2_q, y_q = {}, {}
        for u in range(2):
            round_y(0, gate0[:, :, u * HALF : (u + 1) * HALF], y_stage[u])
            if u == 1:
                w2_q[(0, 1)] = quantise(w2_stage[1], "w2_0_1")
                y_q[(0, 1)] = quantise(y_stage[1], "y_0_1")
            else:
                round_w2(0, 0)
                y_q[(0, 0)] = quantise(y_stage[0], "y_0_0")
                round_w2(0, 1)
                w2_q[(0, 0)] = quantise(w2_stage[0], "w2_0_0")
        for g in range(2):
            round_w2(1, g)
        for g in range(2):
            w2_q[(1, g)] = quantise(w2_stage[g], f"w2_1_{g}")

        def second_stage_pass(acc, b, u, n):
            y_codes, y_scales = y_q[(b, u)]
            codes, scales = w2_q[(b, n // 3)]
            cols = slice((n % 3) * P, (n % 3 + 1) * P)
            nc.tensor.matmul_mx(
                out=acc[:, 0, :],
                lhsT=w4[:, b, 2 * n * P : 2 * (n + 1) * P].bitcast(FP4X4),
                lhsT_scale=w4_sc[:, b, n * P : (n + 1) * P],
                rhs=y_codes[:].bitcast(FP8X4),
                rhs_scale=y_scales[:],
                start=(b == 0),
                stop=False,
            )
            nc.tensor.matmul_mx(
                out=acc[:, 1, :],
                lhsT=codes[:, cols].bitcast(FP8X4),
                lhsT_scale=scales[:, cols],
                rhs=y_codes[:].bitcast(FP8X4),
                rhs_scale=y_scales[:],
                start=False,
                stop=(b == HP - 1),
            )

        for u in range(2):
            round_y(1, gate1[u][:], y_last)
            y_q[(1, u)] = quantise(y_last, f"y_1_{u}")
            accs = [psum.tile([P, 2, HALF], F32, name=f"bank{(u * NT + n) % 8}") for n in range(NT)]
            for b in range(HP):
                for n in range(NT):
                    second_stage_pass(accs[n], b, u, n)
            for first, count in STORES[u]:
                res = ring.tile([P, count, HALF], F32, name="res", bufs=7)
                for d in range(count):
                    acc = accs[first + d]
                    side = ring.tile([P, HALF], F32, name="side", bufs=3)
                    nc.scalar.copy(side[:], acc[:, 0, :])
                    nc.vector.tensor_tensor(res[:, d, :], acc[:, 1, :], side[:], ALU.max)
                rows = out[first * P : (first + count) * P, u * HALF : (u + 1) * HALF]
                nc.sync.dma_start(rows.rearrange("(d p) m -> p d m", p=P), res[:])
